import numpy as np
CORES = [0,4,8,12,16,20,24,28]
N = 8
def setup_inputs(rng):
    return {"x": rng.standard_normal((N, 128, 4), dtype=np.float32)}
def reference(x):
    s = np.maximum.accumulate(x, axis=0)
    return {"y": s.astype(x.dtype)}

from concourse.bass import DstId, RemoteDMATransfer

_B = ("dram", [128, 4], "float32")
SCRATCH = {
    "xs": _B,
    "r0": _B, "r1": _B, "r2": _B, "r3": _B,
    "r4": _B, "r5": _B, "r6": _B, "r7": _B,
    "m": _B,
    "res": _B,
}
SEMAPHORES = ["loaded", "sent", "raw", "part", "done", "stored"]

LO, HI, ALL = 0x00FF, 0xFF00, 0xFFFF
MAX = 2


def rank_program(g, core, T, topo):
    S = T.sem

    def to(c):
        rid, pid, _se = topo.addr(c)
        return DstId(rid=rid, pnc=pid)

    def tr(srcs, dst_core, dst_buf, mask, sem):
        if len(srcs) == 1:
            return RemoteDMATransfer(dst_ids=[to(dst_core)], dma_engine_mask=mask, remote_sem=sem,
                                     src=srcs[0][:], dst=dst_buf[:], alu_op=0)
        return RemoteDMATransfer(dst_ids=[to(dst_core)], dma_engine_mask=mask, remote_sem=sem,
                                 srcs=[s[:] for s in srcs], dsts=[dst_buf[:]], alu_op=MAX)

    R = [T["r%d" % i] for i in range(8)]
    rank = T.rank_of(core)

    if rank is not None:
        chip = topo.chip(core)
        near = chip * 8 + 2
        g.sync.dma_start(T.xs[:], T.x[:]).then_inc(S.loaded, 16)
        g.wait_ge(S.loaded, 16)
        if chip < 2:
            far = (chip + 2) * 8 + 2
            g.remote_dma_fused([tr([T.xs], far, R[rank], LO, S.raw),
                                tr([T.xs], near, R[rank], HI, S.raw)], local_sem=S.sent)
        else:
            g.remote_dma_fused([tr([T.xs], near, R[rank], ALL, S.raw)], local_sem=S.sent)
        if rank == 0:
            g.sync.wait_ge(S.sent, 16)
            g.sync.dma_start(T.y[:], T.x[:]).then_inc(S.stored, 16)
        else:
            g.sync.wait_ge(S.done, 8)
            g.sync.dma_start(T.y[:], T.res[:]).then_inc(S.stored, 16)
        g.wait_ge(S.sent, 16)
        g.sync.wait_ge(S.stored, 16)
        return

    if core == 2:
        g.wait_ge(S.raw, 16)
        g.remote_dma_fused([tr([R[0], R[1]], 10, T.m, LO, S.part),
                            tr([R[0], R[1]], 4, T.res, HI, S.done)], local_sem=S.sent)
        g.wait_ge(S.sent, 16)
    elif core == 10:
        g.wait_ge(S.raw, 16)
        g.wait_ge(S.part, 8)
        g.remote_dma_fused([tr([T.m, R[2]], 8, T.res, LO, S.done),
                            tr([T.m, R[2], R[3]], 12, T.res, HI, S.done)], local_sem=S.sent)
        g.wait_ge(S.sent, 16)
    elif core == 18:
        g.wait_ge(S.raw, 48)
        g.remote_dma_fused([tr([R[0], R[1], R[4], R[5]], 26, T.m, LO, S.part)], local_sem=S.sent)
        g.wait_ge(S.part, 8)
        g.remote_dma_fused([tr([T.m, R[0], R[1], R[4]], 16, T.res, LO, S.done),
                            tr([T.m, R[0], R[1], R[4], R[5]], 20, T.res, HI, S.done)], local_sem=S.sent)
        g.wait_ge(S.sent, 24)
    elif core == 26:
        g.wait_ge(S.raw, 48)
        g.remote_dma_fused([tr([R[2], R[3]], 18, T.m, LO, S.part)], local_sem=S.sent)
        g.wait_ge(S.part, 8)
        g.remote_dma_fused([tr([T.m, R[2], R[3], R[6]], 24, T.res, LO, S.done),
                            tr([T.m, R[2], R[3], R[6], R[7]], 28, T.res, HI, S.done)], local_sem=S.sent)
        g.wait_ge(S.sent, 24)
